import numpy as np
CORES = [2,10,18,26,34,42,50,58,66,74,82,90,98,106,114,122]
N = 16
T = 256
ROUTE = [[[14,3],[0,13],[5,1],[5,0],[4,13],[11,4],[13,4],[15,3],[6,14],[14,13],[3,12],[10,2],[7,10],[9,6],[10,15],[15,11],[10,4],[6,7],[15,11],[2,10],[3,5],[2,13],[14,8],[14,8],[13,5],[7,5],[5,1],[8,2],[1,5],[13,12],[1,11],[12,0],[14,1],[8,5],[14,9],[13,3],[9,4],[15,2],[9,15],[10,9],[3,11],[11,5],[4,12],[7,11],[13,7],[10,9],[11,3],[3,1],[8,10],[7,8],[5,7],[15,11],[5,12],[12,14],[14,9],[3,13],[8,2],[4,10],[3,11],[4,5],[11,7],[7,9],[6,8],[8,0],[6,4],[8,14],[3,13],[13,9],[9,5],[10,5],[8,2],[14,5],[6,8],[2,14],[3,7],[1,8],[6,4],[2,13],[15,2],[12,6],[4,6],[11,6],[7,4],[10,13],[4,7],[7,13],[15,8],[3,11],[12,11],[4,8],[9,6],[9,1],[15,0],[8,13],[0,11],[0,4],[7,12],[2,8],[9,7],[1,7],[12,3],[12,2],[10,4],[15,6],[5,3],[7,13],[1,2],[15,9],[2,3],[5,8],[3,9],[0,14],[13,10],[15,11],[5,8],[5,11],[7,3],[14,11],[9,7],[11,10],[6,10],[13,4],[6,0],[14,11],[4,9],[6,11],[15,3],[12,15],[6,4],[9,6],[11,9],[11,12],[9,2],[13,12],[2,5],[2,10],[14,1],[9,13],[3,8],[8,6],[2,3],[9,12],[12,11],[5,4],[15,1],[12,2],[10,12],[2,0],[7,9],[13,3],[4,8],[9,8],[1,11],[12,5],[7,0],[9,0],[1,13],[13,12],[11,1],[1,2],[9,4],[12,1],[5,0],[6,10],[11,10],[6,2],[3,12],[12,1],[0,5],[6,3],[1,0],[4,13],[6,8],[10,6],[15,11],[7,13],[1,0],[3,11],[8,3],[1,14],[11,9],[14,10],[9,13],[11,3],[1,5],[4,0],[3,1],[10,1],[1,14],[10,1],[12,9],[3,10],[1,0],[5,0],[2,14],[10,14],[8,15],[1,14],[14,0],[12,3],[7,6],[10,3],[11,8],[8,2],[6,3],[13,11],[12,15],[13,14],[4,8],[9,2],[2,8],[5,7],[5,1],[11,9],[13,6],[14,7],[15,8],[3,10],[3,4],[15,12],[9,12],[4,10],[11,15],[9,8],[0,6],[11,1],[7,6],[14,9],[11,1],[4,11],[11,7],[8,14],[15,8],[2,12],[2,15],[11,1],[12,10],[12,2],[1,5],[9,0],[13,5],[11,4],[12,4],[2,8],[3,11],[13,8],[7,8],[8,5],[14,0],[6,7],[2,3],[7,5],[15,6],[3,6],[3,15],[14,7]],[[7,12],[4,14],[12,6],[2,5],[0,4],[13,1],[7,3],[6,8],[4,9],[7,3],[3,13],[6,0],[1,14],[11,14],[8,6],[11,13],[8,14],[5,0],[13,2],[4,6],[15,3],[14,1],[9,6],[7,10],[6,10],[3,1],[1,15],[0,1],[3,11],[4,2],[3,2],[2,0],[8,10],[1,8],[9,5],[2,15],[9,3],[7,8],[7,2],[1,10],[1,4],[9,4],[4,10],[7,12],[13,12],[0,13],[0,6],[0,3],[12,13],[10,6],[4,6],[15,9],[4,3],[3,15],[1,13],[11,4],[9,4],[11,0],[14,9],[15,5],[0,7],[4,13],[9,2],[2,5],[15,0],[11,8],[7,15],[1,6],[1,5],[7,13],[9,8],[0,4],[4,12],[0,2],[2,9],[3,13],[5,12],[13,2],[8,7],[0,10],[11,15],[3,8],[13,10],[13,7],[3,2],[11,12],[2,6],[7,0],[14,10],[0,10],[6,10],[11,14],[12,1],[3,8],[11,4],[0,2],[14,4],[10,0],[3,1],[3,6],[0,2],[13,7],[0,6],[11,5],[10,12],[6,11],[12,3],[13,11],[4,15],[1,0],[6,15],[9,8],[9,6],[8,1],[0,15],[7,13],[13,8],[7,8],[8,4],[14,11],[13,4],[1,4],[10,7],[11,10],[10,8],[5,13],[3,9],[15,0],[15,5],[9,14],[5,15],[14,1],[13,11],[0,6],[8,9],[2,10],[13,11],[1,3],[1,5],[14,13],[8,3],[10,8],[1,15],[4,14],[14,8],[13,14],[9,15],[2,10],[8,12],[7,12],[11,7],[3,7],[11,7],[5,14],[11,7],[7,4],[10,8],[7,0],[4,13],[14,4],[6,15],[13,15],[3,14],[14,4],[10,5],[11,5],[14,4],[4,6],[11,1],[9,8],[0,12],[14,10],[1,0],[12,10],[4,12],[7,4],[3,14],[14,1],[12,13],[11,7],[4,9],[4,10],[4,8],[12,1],[8,1],[11,6],[15,3],[6,15],[10,6],[12,2],[12,15],[1,6],[4,6],[7,4],[8,5],[13,4],[8,3],[1,15],[14,15],[6,1],[10,12],[11,10],[10,3],[9,8],[1,14],[2,7],[8,9],[8,12],[8,7],[10,2],[13,0],[9,10],[6,14],[5,9],[15,11],[11,8],[14,9],[15,9],[12,1],[4,0],[12,8],[4,14],[11,1],[6,3],[5,6],[8,4],[0,5],[15,12],[10,9],[14,0],[13,7],[2,1],[14,3],[6,4],[6,2],[3,8],[13,2],[8,7],[15,6],[2,0],[14,5],[5,10],[6,7],[1,3],[2,9],[4,6],[2,11],[10,9],[15,13],[0,8],[6,2],[6,7],[8,3],[5,11],[6,0],[9,0]],[[11,3],[12,15],[1,8],[2,14],[6,7],[7,8],[5,0],[10,4],[7,1],[6,14],[3,7],[12,15],[12,0],[8,2],[13,3],[4,1],[9,2],[9,0],[5,9],[11,9],[3,7],[0,5],[3,15],[6,2],[14,9],[8,1],[3,2],[0,2],[12,6],[6,4],[13,2],[4,1],[7,9],[6,3],[7,1],[7,3],[13,1],[6,12],[15,0],[6,8],[15,4],[15,12],[14,6],[7,12],[10,15],[3,10],[5,4],[0,1],[8,10],[2,8],[0,15],[11,14],[6,10],[9,7],[11,15],[4,6],[14,13],[15,14],[6,15],[8,1],[1,9],[15,11],[8,7],[13,4],[2,14],[7,6],[8,11],[14,11],[2,1],[3,14],[4,6],[1,3],[2,3],[5,7],[15,3],[3,12],[1,15],[7,0],[5,11],[7,5],[10,9],[9,3],[11,14],[7,15],[0,4],[5,8],[15,6],[5,7],[1,6],[3,2],[12,10],[7,9],[11,9],[13,9],[3,11],[8,9],[3,12],[3,7],[5,1],[6,4],[2,4],[7,8],[2,1],[1,11],[13,4],[0,12],[0,3],[11,9],[3,14],[8,5],[6,5],[9,0],[14,13],[3,13],[2,15],[0,12],[15,8],[13,11],[11,8],[3,15],[13,14],[4,11],[4,5],[14,0],[1,11],[10,11],[3,5],[13,9],[3,13],[11,12],[3,1],[5,13],[13,1],[3,14],[7,13],[2,13],[9,14],[15,14],[3,11],[14,6],[0,11],[3,11],[13,11],[0,14],[14,15],[5,12],[2,1],[2,15],[15,11],[12,4],[12,10],[7,14],[8,1],[9,11],[10,4],[7,2],[11,14],[13,15],[12,6],[2,7],[7,1],[10,4],[0,1],[8,1],[15,6],[14,0],[15,1],[1,3],[13,9],[9,11],[2,4],[1,6],[9,8],[8,7],[6,13],[12,10],[12,7],[11,0],[10,15],[8,10],[8,0],[14,11],[1,13],[15,5],[6,13],[12,13],[0,3],[14,4],[12,6],[12,9],[15,7],[7,10],[6,3],[2,5],[9,5],[13,15],[13,12],[1,4],[9,1],[6,10],[6,3],[4,6],[15,4],[2,11],[13,14],[8,14],[14,6],[9,7],[0,10],[13,5],[9,6],[7,10],[4,2],[2,3],[8,2],[15,2],[7,14],[1,10],[2,10],[9,10],[3,7],[1,7],[0,8],[7,9],[15,12],[5,2],[15,1],[9,6],[4,13],[6,4],[12,2],[11,13],[0,8],[10,14],[12,1],[14,1],[15,4],[7,9],[10,12],[1,8],[7,15],[11,13],[6,11],[9,7],[10,15],[4,15],[13,11],[6,1],[9,11],[11,3],[3,10],[5,10],[14,10],[0,15],[7,6],[2,3]],[[10,7],[4,6],[6,9],[0,4],[0,5],[1,13],[0,15],[6,8],[4,5],[14,1],[13,3],[1,6],[5,2],[14,11],[13,12],[11,6],[10,0],[9,5],[1,10],[13,11],[8,7],[12,6],[6,5],[3,5],[13,5],[10,3],[1,12],[4,5],[15,3],[9,14],[14,5],[13,0],[10,1],[5,9],[10,4],[8,13],[5,0],[0,6],[4,2],[11,6],[2,7],[10,2],[9,13],[12,9],[1,0],[2,9],[5,1],[6,9],[3,7],[14,6],[8,12],[6,11],[15,8],[15,1],[8,15],[12,6],[11,9],[2,5],[10,5],[15,9],[3,14],[13,6],[1,3],[4,14],[7,10],[8,1],[15,14],[13,9],[4,7],[1,12],[8,5],[11,15],[15,4],[8,10],[10,12],[3,4],[2,10],[9,5],[2,6],[8,14],[10,13],[11,9],[8,5],[12,8],[7,0],[8,2],[5,13],[1,7],[11,13],[11,5],[7,9],[12,14],[1,15],[10,7],[11,3],[0,12],[4,7],[10,8],[10,13],[2,1],[1,0],[11,13],[12,14],[2,7],[13,10],[6,14],[0,5],[9,10],[11,2],[15,6],[5,1],[14,15],[14,8],[2,1],[8,2],[13,4],[10,14],[1,14],[15,9],[5,15],[8,2],[13,4],[3,8],[0,12],[12,4],[10,6],[4,13],[10,3],[7,11],[14,11],[5,14],[14,15],[8,3],[14,7],[3,2],[7,6],[1,8],[13,14],[10,13],[7,4],[3,7],[12,14],[0,10],[15,6],[6,4],[7,14],[14,4],[11,7],[12,2],[9,11],[9,11],[8,6],[9,5],[3,14],[14,13],[0,12],[15,14],[0,2],[6,3],[14,2],[9,10],[9,3],[11,9],[4,1],[11,0],[11,0],[2,13],[4,10],[0,1],[4,9],[12,2],[5,7],[5,7],[11,5],[14,15],[12,3],[15,9],[12,2],[9,14],[7,0],[1,11],[15,12],[15,14],[3,13],[14,9],[3,1],[3,4],[7,1],[14,12],[6,4],[14,5],[3,2],[4,0],[12,13],[7,5],[3,13],[0,7],[7,13],[3,5],[4,15],[2,15],[7,8],[4,2],[10,2],[13,15],[10,0],[1,13],[5,1],[14,15],[13,9],[10,1],[6,8],[13,2],[9,11],[1,9],[5,6],[11,6],[9,2],[15,8],[0,9],[7,15],[14,5],[0,1],[15,5],[9,5],[13,1],[15,1],[2,3],[15,14],[0,6],[13,3],[4,5],[4,15],[13,4],[2,11],[6,10],[7,0],[11,9],[9,6],[8,3],[4,7],[1,2],[12,11],[15,13],[15,10],[13,12],[2,10],[0,14],[9,15],[13,0],[11,1],[1,3],[10,2],[11,1],[2,1],[4,10]],[[4,11],[14,0],[8,13],[2,7],[15,5],[0,11],[14,0],[10,15],[4,5],[9,13],[3,14],[13,11],[11,12],[6,13],[11,12],[10,14],[6,4],[5,4],[14,1],[11,4],[9,10],[14,8],[11,0],[14,3],[7,3],[10,4],[15,7],[2,6],[13,0],[0,2],[13,12],[1,12],[2,6],[14,11],[1,9],[13,15],[4,8],[15,6],[4,6],[12,10],[7,5],[2,7],[11,2],[9,3],[7,4],[11,15],[5,15],[12,4],[9,13],[2,4],[13,6],[6,12],[11,5],[1,8],[1,8],[13,8],[5,14],[1,6],[8,2],[13,5],[11,2],[6,12],[6,9],[2,4],[1,5],[13,10],[15,8],[15,5],[15,6],[5,15],[6,10],[6,15],[5,6],[8,6],[14,8],[1,7],[15,11],[12,9],[0,7],[1,5],[4,5],[8,7],[4,1],[15,1],[4,1],[4,6],[3,14],[7,3],[9,7],[9,2],[6,11],[3,8],[2,6],[8,13],[8,14],[4,10],[1,3],[9,15],[1,13],[15,8],[0,10],[9,11],[1,12],[2,14],[15,11],[10,8],[12,13],[2,7],[2,11],[0,7],[15,3],[11,15],[11,12],[14,5],[15,4],[3,14],[7,13],[8,3],[13,8],[8,2],[1,10],[12,9],[6,0],[0,11],[12,11],[9,7],[6,2],[4,11],[1,15],[4,5],[13,5],[1,12],[9,7],[11,1],[6,12],[8,6],[7,12],[3,5],[12,0],[8,0],[3,8],[0,14],[7,0],[5,2],[12,3],[4,5],[11,15],[2,8],[1,14],[1,14],[8,0],[5,15],[9,11],[4,3],[14,13],[8,0],[7,11],[8,15],[11,15],[1,10],[8,5],[8,13],[0,15],[2,13],[3,4],[10,15],[5,2],[10,7],[12,4],[12,8],[12,11],[15,0],[15,7],[1,0],[14,13],[8,0],[11,6],[12,9],[1,8],[0,2],[12,5],[4,15],[14,1],[12,14],[9,15],[11,13],[13,5],[13,12],[2,15],[15,9],[15,2],[12,14],[14,12],[3,8],[7,2],[9,4],[1,3],[15,6],[15,10],[5,15],[11,7],[5,0],[8,12],[12,4],[11,1],[0,6],[11,4],[8,6],[8,5],[6,7],[2,6],[15,6],[5,11],[8,11],[12,13],[9,5],[0,15],[10,3],[7,0],[14,3],[4,6],[4,8],[1,5],[14,1],[15,6],[14,8],[8,14],[7,2],[13,15],[0,4],[5,11],[4,15],[7,2],[8,12],[13,7],[5,8],[7,14],[10,9],[0,6],[15,7],[11,5],[5,15],[6,3],[2,9],[10,0],[11,6],[7,8],[5,6],[0,13],[4,8],[10,2],[4,14],[3,15],[3,5],[0,13],[14,15]],[[15,3],[0,12],[0,4],[10,4],[7,10],[5,11],[1,4],[11,9],[6,0],[15,2],[0,1],[1,12],[11,14],[5,13],[7,14],[13,11],[3,8],[6,4],[10,12],[1,7],[15,0],[2,6],[11,9],[8,14],[11,10],[9,1],[0,10],[13,4],[10,15],[9,15],[1,7],[3,10],[0,13],[9,15],[2,6],[13,10],[0,6],[5,8],[3,13],[11,0],[4,0],[4,2],[12,1],[2,11],[8,6],[1,15],[14,3],[5,4],[4,11],[5,1],[7,12],[15,3],[11,15],[15,2],[15,3],[4,8],[12,5],[13,2],[12,6],[9,1],[0,8],[7,4],[9,4],[4,6],[2,15],[5,1],[15,14],[5,2],[3,10],[3,6],[15,8],[14,0],[7,15],[6,1],[2,7],[15,0],[5,13],[13,8],[14,10],[2,9],[0,1],[1,9],[13,11],[15,11],[3,9],[0,1],[3,5],[4,6],[14,5],[6,14],[5,10],[4,0],[12,6],[9,12],[0,4],[2,9],[11,7],[14,4],[6,9],[11,5],[7,12],[9,4],[8,2],[2,9],[0,14],[11,13],[13,14],[13,4],[12,5],[15,14],[13,5],[13,6],[0,13],[9,4],[5,3],[9,10],[6,13],[0,3],[3,4],[8,15],[7,9],[5,11],[11,10],[4,8],[0,5],[6,3],[11,4],[13,11],[15,12],[4,6],[5,6],[15,8],[8,15],[4,10],[14,8],[12,13],[4,13],[10,15],[14,11],[14,12],[12,15],[0,8],[14,1],[8,10],[10,14],[8,1],[7,15],[4,2],[2,4],[11,6],[12,3],[2,3],[11,2],[1,14],[4,6],[5,13],[5,13],[9,13],[7,15],[8,2],[9,7],[6,10],[14,6],[10,11],[0,3],[14,6],[6,10],[3,6],[5,8],[8,9],[8,12],[5,3],[10,4],[12,14],[4,7],[3,11],[6,1],[15,2],[7,13],[12,5],[2,9],[11,4],[8,5],[9,14],[15,7],[1,3],[9,6],[9,10],[12,10],[13,6],[3,4],[9,13],[3,5],[6,5],[13,2],[1,2],[15,12],[6,2],[12,0],[4,9],[12,13],[10,14],[0,1],[5,11],[1,11],[6,13],[2,5],[6,4],[12,15],[0,15],[12,1],[7,9],[11,12],[3,11],[13,1],[1,0],[5,7],[4,6],[9,2],[3,4],[5,15],[9,11],[7,9],[2,7],[15,14],[6,11],[10,5],[9,6],[2,13],[9,15],[5,4],[7,11],[14,12],[2,0],[8,4],[9,5],[8,11],[7,8],[8,3],[14,10],[6,3],[10,4],[13,7],[9,5],[8,11],[14,12],[3,4],[9,6],[1,0],[7,10],[5,6],[4,3],[11,13],[4,6],[15,2],[14,3]],[[2,9],[5,4],[0,8],[4,6],[5,11],[10,0],[12,10],[9,7],[1,13],[0,7],[0,6],[4,14],[3,0],[1,6],[10,9],[12,14],[5,2],[13,7],[1,9],[7,9],[15,6],[2,3],[13,9],[4,7],[4,0],[15,3],[8,1],[0,4],[7,5],[4,10],[4,8],[13,9],[0,2],[14,10],[15,13],[8,5],[8,14],[6,2],[15,1],[15,12],[14,8],[5,1],[13,12],[14,10],[8,0],[8,13],[8,2],[11,14],[13,10],[11,3],[14,2],[8,13],[1,5],[6,12],[1,14],[10,9],[8,10],[11,10],[9,11],[10,15],[8,1],[12,6],[11,12],[4,15],[10,12],[5,7],[2,5],[1,2],[5,14],[5,11],[9,3],[9,3],[7,8],[9,6],[4,11],[6,4],[9,12],[6,13],[14,12],[8,7],[12,8],[5,3],[11,3],[11,13],[7,14],[8,7],[3,2],[3,10],[14,13],[2,11],[3,12],[13,2],[6,3],[11,7],[15,11],[10,14],[8,12],[10,8],[14,7],[15,2],[1,14],[11,8],[0,1],[14,0],[15,8],[3,14],[13,9],[10,2],[7,5],[5,9],[13,6],[12,8],[10,2],[13,15],[14,2],[9,5],[8,7],[8,3],[4,11],[7,4],[1,3],[2,12],[6,8],[9,4],[3,14],[13,3],[12,10],[15,13],[4,11],[14,7],[14,10],[0,7],[15,5],[6,13],[11,14],[9,11],[9,2],[13,1],[12,1],[10,12],[4,12],[2,5],[8,13],[9,15],[3,8],[3,6],[12,7],[13,3],[9,2],[9,12],[13,7],[4,1],[12,4],[3,9],[1,5],[13,8],[0,3],[15,2],[1,2],[8,12],[12,15],[9,8],[1,3],[3,2],[5,10],[2,9],[11,2],[2,7],[11,9],[6,13],[4,8],[7,5],[4,2],[0,9],[2,1],[10,3],[11,12],[2,13],[13,2],[6,3],[13,6],[11,7],[5,10],[14,15],[9,1],[9,0],[13,15],[6,7],[15,12],[2,0],[7,11],[3,1],[14,0],[4,7],[15,9],[15,2],[10,14],[9,5],[8,2],[6,13],[13,2],[1,3],[9,15],[12,11],[0,4],[11,2],[10,4],[7,5],[14,9],[6,10],[8,7],[0,14],[14,8],[11,7],[8,10],[5,11],[8,1],[10,0],[7,6],[0,5],[9,7],[0,3],[14,0],[4,3],[6,11],[5,11],[3,0],[0,1],[11,10],[14,2],[14,1],[10,12],[12,2],[13,3],[14,8],[10,1],[15,9],[5,10],[3,6],[5,1],[3,2],[15,14],[3,4],[10,7],[9,12],[6,9],[15,7],[6,12],[5,8],[9,4],[15,12],[4,1],[11,2],[15,10],[9,15],[4,11]],[[2,7],[9,13],[7,3],[1,12],[13,15],[2,7],[12,11],[14,4],[4,14],[0,11],[2,15],[6,12],[6,15],[10,2],[3,1],[13,5],[5,15],[3,12],[14,4],[1,2],[7,11],[14,5],[15,3],[10,5],[11,0],[11,14],[12,1],[11,6],[7,3],[12,2],[2,9],[3,11],[15,9],[13,2],[8,9],[4,1],[10,12],[3,6],[1,15],[14,9],[13,1],[14,0],[0,1],[12,9],[8,1],[2,15],[3,7],[6,4],[15,8],[11,7],[14,5],[9,7],[2,14],[11,13],[10,2],[7,11],[7,3],[9,15],[13,11],[11,5],[12,11],[7,6],[9,8],[6,5],[6,11],[15,4],[9,4],[10,15],[0,14],[7,0],[9,8],[8,4],[5,14],[15,14],[8,9],[1,11],[9,2],[7,8],[3,2],[13,0],[7,4],[11,5],[15,7],[1,7],[6,3],[13,4],[9,11],[6,5],[8,10],[9,13],[12,10],[8,13],[3,11],[3,15],[12,5],[15,3],[2,3],[7,10],[0,8],[4,7],[2,3],[6,8],[9,6],[8,12],[1,7],[0,7],[13,6],[6,14],[12,5],[3,7],[14,10],[3,10],[3,0],[2,6],[3,13],[1,0],[5,15],[15,2],[1,6],[6,11],[15,14],[2,3],[6,10],[3,12],[15,9],[14,8],[4,0],[4,10],[8,2],[15,3],[10,5],[12,8],[13,10],[0,12],[11,6],[2,10],[6,13],[11,0],[5,3],[11,2],[11,8],[0,14],[0,14],[9,13],[11,4],[10,0],[0,9],[11,3],[11,13],[8,2],[5,9],[4,5],[4,0],[15,3],[0,15],[15,6],[12,1],[11,14],[11,6],[9,10],[12,0],[2,3],[2,7],[10,2],[8,13],[5,12],[13,15],[12,8],[4,10],[6,1],[0,8],[9,2],[2,11],[13,5],[9,0],[9,4],[6,9],[12,14],[6,3],[2,8],[6,2],[2,13],[2,8],[12,7],[6,0],[9,1],[15,6],[1,14],[10,3],[13,6],[8,9],[7,12],[4,10],[15,2],[9,11],[4,13],[15,7],[2,14],[12,15],[10,6],[14,8],[7,11],[10,7],[13,15],[3,12],[1,0],[5,3],[3,9],[14,4],[3,10],[0,2],[7,8],[13,2],[2,12],[7,8],[15,8],[12,7],[8,0],[15,5],[11,1],[2,9],[12,6],[14,2],[7,15],[4,6],[6,14],[9,15],[5,14],[11,7],[3,10],[12,2],[3,14],[12,6],[6,8],[7,11],[8,5],[10,0],[0,7],[15,9],[4,15],[9,12],[3,14],[5,7],[10,8],[14,10],[6,11],[11,0],[10,1],[5,13],[1,13],[5,7],[3,1],[8,6],[14,13],[14,3],[2,11]],[[2,0],[10,0],[13,0],[2,1],[1,15],[7,1],[9,6],[1,0],[12,6],[3,11],[12,15],[0,13],[0,5],[7,5],[5,11],[8,6],[4,15],[8,0],[6,0],[5,9],[10,13],[7,9],[14,12],[1,8],[9,2],[2,4],[8,6],[6,9],[15,8],[9,14],[3,13],[8,7],[3,12],[7,6],[1,7],[1,14],[5,6],[6,0],[10,15],[14,8],[14,2],[3,11],[10,9],[0,8],[2,9],[13,14],[4,8],[4,5],[3,9],[7,5],[11,13],[14,8],[3,9],[9,13],[2,3],[4,7],[6,0],[15,4],[15,14],[7,14],[0,3],[12,9],[10,3],[15,7],[2,0],[14,5],[11,1],[14,8],[3,12],[8,4],[3,0],[7,3],[14,12],[8,7],[13,6],[1,3],[2,15],[6,14],[12,3],[14,11],[11,0],[14,12],[15,6],[7,6],[3,5],[9,1],[12,2],[10,15],[5,4],[7,0],[6,4],[1,12],[1,12],[0,7],[13,1],[10,12],[3,14],[15,4],[11,4],[2,6],[3,7],[8,15],[7,3],[0,5],[6,0],[10,8],[11,13],[7,8],[2,9],[14,2],[12,1],[11,5],[15,8],[3,13],[15,4],[6,0],[9,3],[6,12],[12,9],[1,2],[11,6],[4,12],[0,13],[6,12],[3,7],[2,12],[6,10],[6,11],[6,5],[11,7],[6,14],[4,5],[0,10],[12,10],[13,12],[9,13],[5,3],[4,6],[1,2],[0,4],[9,10],[12,2],[8,2],[4,10],[6,3],[15,4],[2,3],[7,5],[0,8],[5,8],[11,0],[9,15],[14,13],[10,1],[13,12],[11,8],[8,3],[0,14],[0,9],[8,6],[0,8],[14,0],[8,9],[7,9],[1,15],[15,3],[10,15],[2,13],[0,15],[10,3],[9,15],[3,13],[11,3],[8,6],[0,13],[10,1],[8,14],[12,14],[10,5],[11,14],[11,12],[11,3],[11,13],[6,2],[8,13],[1,9],[13,14],[1,0],[12,4],[14,12],[3,15],[5,7],[9,10],[1,14],[13,3],[6,7],[10,2],[11,5],[6,13],[11,2],[15,12],[4,15],[6,2],[6,1],[11,3],[4,1],[13,7],[10,14],[11,4],[3,6],[12,10],[7,0],[12,6],[4,6],[10,14],[2,10],[14,11],[5,2],[4,8],[13,10],[5,2],[15,7],[5,2],[11,0],[9,2],[9,11],[13,5],[11,1],[13,0],[11,6],[9,3],[7,11],[3,4],[8,13],[8,6],[8,6],[14,12],[1,15],[10,14],[12,2],[5,12],[11,5],[0,8],[8,6],[5,0],[15,9],[13,4],[14,8],[7,2],[9,15],[6,1],[6,2],[9,13],[15,2],[1,7],[11,8]],[[13,8],[12,15],[3,13],[13,11],[14,2],[5,7],[3,8],[0,9],[6,7],[1,4],[3,12],[15,7],[1,5],[8,2],[12,6],[12,15],[12,5],[13,4],[10,5],[6,8],[2,8],[2,4],[13,11],[1,14],[1,15],[12,4],[0,9],[11,3],[1,3],[2,1],[12,11],[3,2],[0,8],[4,7],[15,14],[15,13],[8,9],[10,5],[5,9],[6,3],[7,8],[9,1],[10,3],[11,9],[11,15],[1,5],[0,8],[11,10],[4,10],[15,7],[15,5],[12,4],[0,10],[14,2],[2,10],[7,10],[13,10],[1,0],[13,5],[3,12],[10,9],[11,15],[6,12],[0,5],[7,14],[15,8],[15,14],[14,0],[2,9],[1,8],[6,10],[5,8],[4,10],[14,6],[15,8],[1,6],[3,8],[10,8],[1,13],[8,15],[2,4],[3,14],[10,5],[11,1],[10,12],[1,12],[7,5],[5,10],[11,6],[13,11],[11,2],[14,3],[3,2],[15,9],[11,9],[10,2],[10,8],[1,5],[11,13],[9,11],[2,1],[4,14],[1,12],[15,6],[0,11],[13,12],[9,10],[10,2],[8,2],[11,5],[5,14],[14,15],[13,7],[7,2],[14,15],[9,3],[5,6],[12,2],[12,0],[11,9],[10,7],[5,4],[1,6],[7,15],[2,9],[13,15],[5,11],[12,9],[8,10],[7,6],[0,6],[12,7],[0,5],[0,6],[2,3],[5,14],[1,13],[13,0],[6,10],[10,5],[10,7],[11,7],[15,11],[4,7],[14,6],[4,8],[7,11],[4,5],[10,12],[1,9],[15,5],[5,14],[9,1],[7,8],[11,0],[1,11],[12,2],[13,6],[1,3],[12,3],[9,3],[13,0],[7,11],[3,8],[4,10],[10,6],[4,1],[7,11],[9,0],[11,2],[7,2],[9,0],[14,5],[7,3],[2,4],[3,5],[13,4],[4,0],[1,13],[1,4],[8,9],[14,12],[2,6],[2,3],[2,0],[7,2],[6,15],[15,1],[12,2],[14,15],[11,15],[4,11],[12,14],[5,9],[3,6],[5,9],[7,0],[9,4],[2,11],[14,12],[2,0],[7,9],[12,2],[13,8],[1,13],[15,0],[6,4],[0,1],[2,7],[15,2],[15,12],[9,8],[11,14],[11,12],[10,6],[10,11],[8,2],[0,14],[2,14],[12,13],[13,6],[6,13],[15,9],[4,5],[10,13],[12,11],[3,8],[3,15],[15,0],[2,1],[11,6],[15,11],[11,7],[8,5],[5,2],[9,3],[6,15],[6,7],[0,9],[11,1],[15,14],[8,11],[2,0],[2,13],[5,1],[5,4],[8,5],[4,11],[12,8],[12,5],[14,7],[10,5],[9,13],[1,9],[15,14],[12,3]],[[4,9],[9,0],[12,11],[12,1],[3,14],[15,3],[4,12],[4,13],[9,4],[6,4],[8,13],[8,14],[4,0],[9,0],[3,10],[10,5],[5,4],[9,3],[7,11],[10,7],[2,5],[6,14],[8,15],[4,10],[3,5],[4,15],[1,12],[7,13],[13,0],[2,12],[9,11],[15,14],[8,4],[0,3],[9,11],[7,1],[13,9],[3,9],[13,3],[9,15],[3,12],[5,7],[1,7],[7,6],[0,7],[2,1],[3,8],[1,7],[12,13],[1,15],[0,12],[12,5],[2,7],[8,2],[0,13],[1,11],[11,13],[6,2],[15,14],[5,10],[14,0],[3,1],[6,9],[0,7],[13,0],[4,5],[5,13],[13,0],[10,3],[11,13],[15,11],[5,6],[5,6],[2,3],[11,15],[7,6],[15,5],[11,5],[5,7],[6,2],[1,14],[11,14],[14,9],[6,11],[14,11],[2,4],[13,7],[5,2],[7,5],[2,13],[8,14],[8,2],[4,8],[10,6],[7,8],[7,13],[5,9],[15,3],[13,10],[4,2],[13,6],[11,1],[11,8],[0,5],[5,13],[12,10],[4,14],[2,8],[10,12],[4,15],[2,10],[10,5],[12,9],[3,14],[12,3],[0,5],[9,11],[0,4],[5,14],[5,2],[5,12],[0,7],[7,2],[0,2],[10,3],[13,11],[1,5],[3,0],[11,14],[10,8],[8,1],[2,3],[14,12],[1,13],[3,15],[15,3],[1,9],[10,0],[8,12],[2,10],[11,3],[10,1],[8,0],[15,9],[11,9],[8,5],[11,7],[7,14],[6,14],[1,4],[9,14],[2,5],[15,2],[1,3],[2,5],[15,0],[12,0],[3,11],[9,12],[0,3],[10,11],[1,10],[13,9],[11,4],[2,9],[0,3],[12,8],[9,10],[5,2],[4,13],[8,15],[0,6],[0,7],[8,9],[13,14],[0,11],[8,13],[2,0],[0,7],[1,11],[2,13],[15,9],[6,1],[13,0],[0,7],[4,13],[7,4],[11,2],[11,1],[5,10],[5,14],[3,9],[2,15],[13,11],[1,10],[13,3],[10,12],[4,9],[8,1],[5,1],[0,8],[0,7],[11,4],[14,13],[11,0],[15,0],[2,14],[12,1],[5,9],[2,10],[0,12],[8,6],[8,9],[2,3],[5,2],[10,5],[13,2],[3,2],[10,13],[11,1],[15,14],[10,9],[0,1],[1,14],[8,10],[10,8],[3,0],[12,1],[12,1],[10,7],[15,0],[12,5],[7,14],[3,4],[6,15],[8,3],[8,6],[11,2],[8,7],[1,8],[4,15],[3,1],[11,14],[14,6],[9,14],[6,15],[1,11],[0,7],[10,4],[7,12],[11,14],[11,3],[0,14],[13,10],[9,6],[11,2]],[[13,15],[9,15],[3,14],[11,7],[12,1],[3,6],[4,6],[13,5],[1,14],[4,6],[3,9],[5,8],[2,13],[12,0],[8,13],[0,14],[13,0],[6,3],[8,15],[14,0],[4,2],[15,6],[4,6],[6,13],[13,12],[15,12],[15,9],[11,9],[6,12],[5,9],[7,11],[13,3],[12,6],[10,7],[6,5],[2,15],[3,5],[8,3],[6,7],[1,8],[3,1],[2,12],[7,9],[6,13],[12,6],[9,7],[6,15],[9,14],[9,0],[3,11],[1,4],[2,3],[2,5],[11,6],[9,14],[6,4],[4,10],[15,13],[7,13],[4,3],[4,10],[5,2],[1,5],[5,13],[7,4],[10,1],[11,7],[1,3],[4,7],[15,6],[6,13],[3,11],[9,0],[8,10],[14,3],[1,10],[5,1],[2,5],[3,13],[3,14],[11,0],[0,1],[0,10],[4,3],[11,10],[10,11],[0,15],[2,13],[6,10],[5,10],[7,5],[11,12],[6,3],[11,15],[11,8],[6,14],[14,5],[7,2],[6,15],[1,12],[0,8],[3,10],[7,10],[12,6],[3,5],[14,6],[2,4],[13,6],[1,14],[1,4],[2,3],[1,13],[7,14],[3,0],[11,9],[7,13],[6,14],[7,9],[4,0],[7,6],[2,8],[4,11],[11,8],[6,12],[10,7],[14,12],[2,15],[2,11],[9,7],[10,13],[1,4],[13,12],[13,14],[14,9],[14,7],[10,5],[7,0],[13,8],[4,5],[1,7],[12,15],[4,0],[6,14],[2,0],[9,10],[15,7],[11,6],[8,2],[3,4],[6,11],[9,6],[7,5],[10,11],[14,4],[3,10],[8,11],[6,3],[8,3],[2,15],[15,14],[1,15],[2,9],[1,14],[5,3],[12,0],[6,8],[0,10],[12,4],[12,5],[0,15],[8,11],[12,0],[1,6],[12,1],[9,14],[10,5],[2,4],[8,4],[13,4],[11,12],[9,13],[4,11],[1,9],[15,14],[6,1],[5,4],[9,4],[9,3],[0,2],[10,6],[9,15],[6,8],[2,7],[9,4],[5,14],[13,15],[3,8],[3,10],[1,11],[8,5],[13,14],[9,8],[5,7],[7,14],[14,6],[8,13],[13,9],[13,6],[14,12],[7,12],[0,9],[2,5],[11,7],[5,1],[12,6],[15,3],[10,3],[5,6],[2,14],[12,10],[5,1],[9,3],[10,7],[7,14],[14,12],[5,1],[7,10],[1,13],[0,2],[3,6],[15,0],[6,15],[8,3],[0,3],[1,4],[3,10],[5,11],[12,9],[2,0],[4,13],[1,6],[5,14],[6,13],[14,5],[13,11],[7,6],[14,12],[3,0],[15,1],[3,12],[7,11],[13,11],[13,6],[11,15],[14,12],[13,5]],[[5,2],[13,10],[10,0],[2,0],[10,0],[8,12],[5,4],[13,10],[2,12],[9,12],[5,0],[12,6],[11,13],[13,0],[12,14],[5,9],[10,13],[8,14],[6,8],[3,5],[4,8],[7,0],[11,4],[10,1],[11,0],[6,13],[10,8],[3,14],[12,15],[12,11],[2,4],[2,1],[12,0],[9,8],[3,8],[2,8],[11,6],[8,15],[12,9],[4,7],[9,6],[1,4],[15,10],[9,11],[8,5],[3,2],[12,11],[6,13],[7,3],[14,5],[8,12],[0,9],[3,2],[3,11],[4,2],[8,5],[5,1],[12,3],[13,2],[15,9],[14,6],[2,6],[10,9],[8,4],[8,13],[8,14],[5,7],[7,0],[15,9],[0,15],[9,5],[13,1],[13,0],[13,0],[11,14],[14,3],[15,3],[7,2],[6,2],[11,13],[12,5],[1,15],[9,6],[3,1],[13,12],[14,5],[10,14],[4,3],[13,12],[12,8],[0,14],[12,9],[10,7],[10,1],[13,12],[0,5],[15,0],[6,2],[14,13],[14,10],[8,4],[13,7],[13,1],[3,8],[7,0],[14,8],[5,10],[2,8],[13,3],[8,2],[2,0],[9,10],[10,13],[3,0],[12,7],[4,15],[14,9],[6,13],[8,5],[11,0],[8,0],[7,1],[3,6],[13,5],[6,13],[6,3],[2,7],[9,8],[14,3],[1,15],[14,15],[10,13],[8,11],[3,2],[14,8],[2,11],[0,13],[14,8],[11,15],[8,4],[2,13],[8,10],[1,6],[3,15],[11,5],[6,9],[13,1],[13,6],[3,4],[2,7],[9,1],[7,15],[6,7],[6,13],[3,8],[3,12],[9,15],[10,8],[4,0],[3,10],[0,7],[15,10],[14,15],[11,5],[12,11],[9,1],[1,5],[11,8],[11,5],[3,0],[4,12],[15,2],[2,8],[9,7],[8,11],[6,3],[13,3],[11,4],[7,8],[6,5],[2,14],[12,4],[9,0],[8,9],[13,4],[8,1],[6,4],[12,13],[13,10],[8,6],[1,15],[13,9],[7,8],[14,2],[15,12],[14,8],[14,5],[10,7],[7,0],[8,14],[15,10],[9,6],[8,3],[4,2],[4,6],[11,2],[15,2],[7,8],[13,6],[15,3],[12,5],[9,6],[15,6],[9,15],[0,2],[14,5],[7,2],[11,12],[12,4],[4,9],[4,5],[3,10],[14,10],[1,2],[6,1],[1,6],[14,13],[7,5],[6,3],[10,1],[14,2],[8,14],[8,13],[7,14],[13,4],[5,7],[5,14],[9,12],[5,8],[9,14],[1,9],[8,2],[3,2],[9,5],[10,7],[10,12],[1,2],[2,1],[11,10],[13,1],[4,6],[7,9],[3,12],[8,9],[15,13],[13,1]],[[11,15],[15,3],[12,14],[7,6],[14,15],[8,14],[5,12],[5,12],[2,1],[15,4],[10,14],[14,0],[11,15],[14,1],[12,7],[9,12],[2,9],[4,9],[9,2],[3,8],[10,1],[9,14],[6,5],[4,1],[8,5],[4,1],[3,6],[14,3],[5,8],[8,9],[6,4],[5,4],[3,9],[14,2],[6,1],[3,5],[3,4],[0,3],[4,5],[9,7],[4,0],[10,11],[5,2],[7,8],[15,5],[12,11],[15,7],[0,9],[0,15],[2,15],[4,9],[11,7],[6,4],[14,15],[2,11],[11,12],[8,6],[13,9],[2,9],[5,13],[7,3],[3,8],[6,4],[9,2],[5,1],[13,6],[8,10],[11,5],[7,2],[9,0],[15,2],[6,2],[11,0],[1,3],[4,5],[8,14],[14,13],[4,2],[1,11],[12,8],[6,12],[14,8],[1,7],[11,12],[11,14],[6,7],[5,14],[1,4],[0,1],[15,12],[3,11],[7,9],[3,0],[15,14],[11,4],[3,6],[4,5],[3,0],[8,7],[3,0],[8,13],[15,4],[5,2],[4,0],[4,12],[3,2],[15,11],[0,9],[14,9],[3,15],[10,14],[4,14],[0,12],[9,1],[10,7],[9,14],[12,4],[0,5],[12,13],[3,1],[5,14],[2,14],[8,12],[8,3],[14,10],[13,11],[3,8],[11,13],[6,13],[13,11],[4,10],[0,6],[2,3],[14,2],[14,1],[8,0],[5,9],[10,2],[10,12],[7,4],[1,8],[5,8],[12,15],[11,8],[12,0],[11,1],[15,7],[10,0],[14,7],[14,12],[1,2],[9,12],[12,4],[5,12],[8,2],[10,0],[1,5],[15,11],[13,2],[8,2],[15,8],[11,5],[14,15],[15,1],[5,9],[10,5],[3,9],[2,15],[4,2],[15,2],[6,10],[1,7],[13,0],[8,11],[12,6],[12,2],[14,10],[11,5],[13,7],[15,3],[8,13],[2,3],[9,2],[12,14],[4,6],[14,4],[15,14],[12,3],[14,10],[1,12],[1,11],[13,7],[11,0],[6,11],[6,3],[12,2],[4,10],[6,8],[1,15],[1,4],[3,14],[5,3],[6,1],[14,13],[13,2],[9,1],[5,7],[9,7],[12,4],[15,13],[13,10],[8,11],[14,2],[6,9],[9,3],[0,2],[10,5],[0,10],[12,13],[11,6],[8,14],[2,11],[15,4],[1,7],[8,1],[11,1],[0,4],[11,7],[8,15],[6,14],[13,14],[1,15],[15,0],[5,15],[2,6],[14,4],[0,15],[11,0],[15,13],[11,0],[8,2],[14,7],[10,1],[14,6],[5,4],[14,15],[12,2],[11,1],[13,5],[6,10],[6,10],[13,0],[9,11],[4,1],[10,8],[8,14]],[[8,7],[12,0],[10,11],[15,6],[1,3],[15,10],[15,14],[2,11],[10,1],[3,10],[1,0],[5,1],[15,9],[11,3],[0,10],[12,7],[2,1],[15,4],[14,15],[13,1],[11,8],[12,4],[9,1],[15,6],[13,6],[5,2],[15,1],[4,13],[11,3],[8,6],[10,3],[4,12],[13,3],[12,2],[3,13],[7,15],[6,8],[3,13],[9,4],[15,7],[1,14],[10,8],[15,14],[9,14],[4,15],[2,8],[7,13],[4,15],[15,4],[11,5],[8,14],[4,11],[5,15],[9,4],[10,7],[5,11],[9,13],[15,13],[5,15],[14,10],[5,4],[5,8],[8,1],[7,0],[6,4],[1,7],[5,1],[14,0],[6,4],[8,7],[5,11],[12,6],[6,13],[3,4],[10,12],[13,4],[5,13],[11,7],[15,2],[2,12],[14,1],[7,4],[2,12],[3,0],[2,7],[9,6],[13,10],[13,3],[12,9],[1,14],[12,9],[3,10],[13,7],[11,5],[13,2],[14,3],[13,7],[6,7],[7,3],[10,3],[14,1],[1,4],[13,10],[11,3],[11,0],[11,6],[8,10],[12,11],[7,11],[1,8],[2,7],[11,2],[4,6],[1,14],[1,7],[2,0],[5,3],[3,11],[13,7],[6,11],[4,11],[11,7],[3,12],[1,14],[15,14],[4,6],[11,0],[4,1],[7,6],[10,7],[5,8],[13,4],[6,8],[3,1],[8,11],[10,2],[8,15],[2,9],[12,6],[2,8],[12,11],[5,6],[0,6],[9,10],[12,14],[2,8],[13,9],[1,0],[14,8],[2,5],[6,5],[15,14],[14,8],[4,10],[10,11],[1,9],[0,9],[13,14],[4,11],[13,6],[7,11],[5,11],[3,10],[4,8],[14,1],[7,15],[11,0],[9,6],[12,1],[3,7],[5,0],[5,8],[13,14],[13,11],[15,7],[13,1],[2,13],[9,13],[7,12],[2,10],[10,14],[15,0],[12,6],[4,3],[9,4],[9,2],[15,0],[15,11],[7,11],[5,2],[10,9],[11,1],[3,15],[1,3],[12,0],[4,14],[15,11],[6,7],[3,5],[12,15],[8,5],[7,13],[0,8],[10,14],[4,5],[15,13],[1,8],[10,2],[6,13],[2,5],[1,5],[4,9],[13,0],[7,2],[8,5],[1,2],[11,6],[0,10],[13,11],[11,14],[15,4],[15,1],[10,15],[4,1],[13,15],[9,6],[13,10],[7,0],[5,14],[2,4],[11,5],[1,9],[9,7],[0,9],[1,10],[10,2],[6,15],[1,12],[13,10],[8,4],[0,9],[2,11],[7,10],[6,1],[7,0],[8,5],[6,8],[9,1],[7,12],[15,6],[15,12],[3,5],[2,0],[10,12],[0,2],[6,5]],[[15,9],[14,4],[12,14],[10,4],[6,10],[0,1],[12,14],[7,2],[6,3],[4,6],[11,6],[0,4],[14,3],[4,1],[7,0],[4,0],[12,4],[1,8],[4,14],[12,15],[3,8],[13,15],[5,1],[6,0],[5,12],[5,0],[9,15],[4,9],[0,9],[8,12],[10,9],[6,7],[8,2],[1,11],[1,4],[15,2],[12,10],[13,1],[4,14],[2,8],[9,8],[10,11],[3,11],[4,0],[0,10],[7,11],[14,2],[8,3],[1,7],[7,1],[0,14],[6,8],[0,4],[13,6],[9,4],[3,6],[13,2],[2,14],[11,9],[13,5],[7,1],[7,8],[4,1],[11,12],[4,0],[3,4],[3,1],[0,9],[6,1],[9,5],[9,5],[6,14],[15,2],[13,2],[4,11],[13,4],[1,11],[1,6],[9,13],[4,5],[12,2],[11,4],[5,3],[14,3],[14,6],[3,10],[0,11],[1,4],[14,7],[1,3],[8,0],[7,12],[2,8],[3,7],[13,0],[12,10],[10,15],[11,3],[11,14],[13,7],[6,9],[6,10],[10,3],[15,5],[14,12],[4,13],[14,7],[8,11],[15,9],[8,2],[3,7],[4,11],[7,5],[5,10],[5,8],[4,10],[9,4],[1,2],[7,2],[0,11],[15,4],[3,4],[7,5],[6,12],[3,0],[7,15],[9,6],[1,0],[6,3],[13,2],[6,14],[14,0],[3,13],[12,3],[4,8],[9,12],[7,2],[5,0],[2,7],[13,10],[1,14],[7,11],[11,4],[4,10],[0,2],[6,9],[6,11],[13,8],[4,14],[1,5],[11,8],[7,12],[1,8],[13,15],[8,2],[1,5],[6,2],[5,7],[3,2],[11,10],[11,0],[0,8],[9,13],[9,0],[1,2],[2,0],[9,12],[0,6],[0,5],[7,4],[11,0],[4,5],[5,11],[2,9],[2,12],[11,14],[1,5],[0,9],[10,1],[2,4],[7,11],[1,4],[12,3],[0,14],[6,14],[2,12],[13,14],[10,4],[1,2],[2,7],[10,2],[3,2],[10,9],[8,7],[7,8],[14,6],[1,8],[14,0],[14,4],[14,2],[13,2],[10,0],[15,6],[0,11],[6,3],[13,3],[10,4],[13,2],[1,3],[14,5],[10,8],[13,2],[7,8],[2,14],[7,9],[6,14],[1,8],[10,13],[13,10],[1,13],[3,14],[0,3],[9,13],[6,1],[15,6],[1,14],[3,11],[0,13],[8,15],[5,9],[2,6],[0,6],[12,1],[7,6],[15,4],[12,9],[1,13],[12,7],[8,15],[6,10],[10,1],[7,6],[7,11],[4,8],[2,12],[15,2],[5,4],[9,13],[2,4],[10,6],[2,12],[3,11],[10,13],[2,8],[11,7],[15,11]]]
YW = 552
def setup_inputs(rng):
    return {"x": rng.standard_normal((N, 128, T), dtype=np.float32)}
def reference(x):
    y = np.full((N, 128, YW), np.nan, x.dtype)
    fill = [0] * N
    for r in range(N):
        for t in range(T):
            for e in ROUTE[r][t]:
                y[e][:, fill[e]] = x[r][:, t]
                fill[e] += 1
    return {"y": y}

from concourse.bass import DstId, RemoteDMATransfer

NR = 16
NT = 256
RK = 2
FOUR = 0

SCRATCH = {
    "xs": ("sbuf", [128, 256], "float32"),
    "st0": ("sbuf", [128, 64], "float32"),
    "st1": ("sbuf", [128, 64], "float32"),
    "land": ("sbuf", [128, 552], "float32"),
}
SEMAPHORES = ["loaded", "chunk", "packed", "arrived", "stored", "sent"]

CACHE = {}


def tables(route):
    if "tab" in CACHE:
        return CACHE["tab"]
    n = [[0] * NR for _ in range(NR)]
    pos = [{} for _ in range(NR)]
    for r in range(NR):
        for t in range(NT):
            for e in route[r][t]:
                pos[r][(t, e)] = n[r][e]
                n[r][e] += 1
    off = [[0] * (NR + 1) for _ in range(NR)]
    for e in range(NR):
        for r in range(NR):
            off[e][r + 1] = off[e][r] + n[r][e]
    CACHE["tab"] = (n, off, pos)
    return CACHE["tab"]


def stage_map(r, n):
    cross = [[], []]
    same = [[], []]
    for e in range(NR):
        if e == r:
            continue
        c = ((r >> 1) + (e >> 1)) & 1
        (cross if (e ^ r) & 1 else same)[c].append(e)
    amap = {}
    for lst, cores in ((cross[0], (2, 3)), (cross[1], (6, 7)), (same[0], (0, 1)), (same[1], (4, 5))):
        lst = sorted(lst, key=lambda e: (-n[r][e], e))
        load = [0, 0]
        cnt = [0, 0]
        for e in lst:
            i = 0 if (cnt[0] < 2 and (load[0] <= load[1] or cnt[1] >= 2)) else 1
            amap[e] = (cores[i], cnt[i])
            cnt[i] += 1
            load[i] += n[r][e]
    amap[r] = (RK, 2)
    return amap


def analyse(rt, amap, k, b0, b1):
    units = {}
    for t in range(b0, b1):
        for e in rt[t]:
            units.setdefault(e, []).append(t)
    loc = []
    single = {}
    pairs = []
    for e in sorted(units):
        runs = []
        for t in units[e]:
            if runs and runs[-1][0] + runs[-1][1] == t:
                runs[-1][1] += 1
            else:
                runs.append([t, 1])
        if amap[e][0] == k:
            loc += [(t, ln, e) for t, ln in runs]
            continue
        for t, ln in runs:
            while ln >= 2:
                pairs.append((t, [e]))
                t += 2
                ln -= 2
            if ln:
                single.setdefault(t, []).append(e)
    heavy = [(t, single[t]) for t in sorted(single) if len(single[t]) == 2]
    light = [(t, single[t]) for t in sorted(single) if len(single[t]) == 1]
    return heavy, light, pairs, loc


def p2(x):
    m = 1
    while m * 2 <= x and m < 16:
        m *= 2
    return m


def cost(nh, nl, npr, four):
    best = None
    for hk in range(min(nh, 16), -1, -1):
        lp = nl + 2 * (nh - hk)
        c = 16 - hk
        l2 = lp - min(lp, 2 * c)
        q2 = npr - min(npr, c)
        rem = l2 + q2 - hk
        if rem <= 0:
            if best is None or 384 < best[0]:
                best = (384, hk, 0, 0)
            continue
        for r2 in range(max(0, rem - l2), min(rem, q2) + 1):
            r1 = rem - r2
            a = l2 - r1
            b = q2 - r2
            if r2 and a < r2:
                continue
            d2 = 128 // p2(a // r2) if r2 else 0
            if four:
                if r1 > 16:
                    continue
                d1 = 128 // p2(16 // r1) if r1 else 0
                m = 384 + d1 + d2
            else:
                if r1 and b < r1:
                    continue
                d1 = 128 // p2(b // r1) if r1 else 0
                m = 384 + max(d1, d2)
            if best is None or m < best[0]:
                best = (m, hk, r1, r2)
    return best


def bounds(rt, amap, four):
    f = [{0: (0, None)}]
    for k in range(8):
        g = {}
        for b0 in sorted(f[-1]):
            v = f[-1][b0][0]
            for b1 in range(b0 + 24, min(NT, b0 + 42) + 1):
                if (k == 7 and b1 != NT) or (k < 7 and abs(b1 - 32 * (k + 1)) > 10):
                    continue
                heavy, light, pairs, loc = analyse(rt, amap, k, b0, b1)
                cc = cost(len(heavy), len(light), len(pairs), four)
                if cc is None:
                    continue
                c = max(v, cc[0] + 8 * len(loc))
                if b1 not in g or c < g[b1][0]:
                    g[b1] = (c, b0)
        f.append(g)
    if NT not in f[8]:
        return [32 * k for k in range(9)]
    b = [NT]
    for k in range(8, 0, -1):
        b.append(f[k][b[-1]][1])
    return b[::-1]


def bits(engs):
    m = 0
    for j in engs:
        m |= 1 << j
    return m


def schedule(heavy, light, pairs, four):
    cc = cost(len(heavy), len(light), len(pairs), four)
    if cc is None:
        calls = []
        for w, lst in ((1, heavy + light), (2, pairs)):
            for i in range(0, len(lst), 16):
                calls.append((w, [(t, es, [j]) for j, (t, es) in enumerate(lst[i:i + 16])]))
        return calls
    hk, r1, r2 = cc[1], cc[2], cc[3]
    s0, s1, s2, pc = [], [], [], []
    lights = list(light)
    for t, es in heavy[hk:]:
        lights += [(t, [es[0]]), (t, [es[1]])]
    prs = list(pairs)
    for j in range(hk):
        s0.append((heavy[j][0], heavy[j][1], [j]))
    for j in range(hk, 16):
        if lights:
            t, es = lights.pop()
            s0.append((t, es, [j]))
        if lights:
            t, es = lights.pop()
            s1.append((t, es, [j]))
        if prs:
            t, es = prs.pop()
            pc.append((t, es, [j]))
    a = len(lights) - r1
    j = 0
    for _ in range(a):
        t, es = lights.pop()
        s1.append((t, es, [j]))
        j += 1
    for _ in range(len(prs) - r2):
        t, es = prs.pop()
        pc.append((t, es, [j]))
        j += 1
    if r2:
        m = p2(a // r2)
        for i in range(r2):
            t, es = prs.pop()
            pc.append((t, es, list(range(i * m, i * m + m))))
    if r1:
        if four:
            m = p2(16 // r1)
            for i in range(r1):
                t, es = lights.pop()
                s2.append((t, es, list(range(i * m, i * m + m))))
        else:
            m = p2((hk - a) // r1)
            for i in range(r1):
                t, es = lights.pop()
                s1.append((t, es, list(range(a + i * m, a + i * m + m))))
    return [(w, c) for w, c in ((1, s0), (1, s1), (2, pc), (1, s2)) if c]


def plan(r, route):
    if r in CACHE:
        return CACHE[r]
    n, off, pos = tables(route)
    rt = route[r]
    amap = stage_map(r, n)
    b = bounds(rt, amap, FOUR)

    def place(t, e):
        k, slot = amap[e]
        if e == r:
            return k, "land", off[r][r] + pos[r][(t, e)]
        return k, "st%d" % slot, pos[r][(t, e)]

    calls = []
    locs = []
    packed = [0] * 8
    for k in range(8):
        heavy, light, pairs, loc = analyse(rt, amap, k, b[k], b[k + 1])
        cl = []
        for w, trs in schedule(heavy, light, pairs, FOUR):
            out = []
            for t, es, engs in trs:
                dsts = [place(t, e) for e in es]
                for d in dsts:
                    packed[d[0]] += len(engs)
                out.append((t, bits(engs), len(engs), dsts))
            cl.append((w, out))
        calls.append(cl)
        locs.append([(t, ln) + place(t, e)[1:] for t, ln, e in loc])
        packed[k] += 16 * len(loc)
    width = max(b[k + 1] - b[k] for k in range(8) if k != RK)
    win = [min(b[k], NT - width) for k in range(8)]
    sends = [[] for _ in range(8)]
    for e in range(NR):
        if e != r:
            sends[amap[e][0]].append((amap[e][1], e, n[r][e]))
    CACHE[r] = {"calls": calls, "locs": locs, "packed": packed, "width": width, "win": win, "sends": sends}
    return CACHE[r]


def rank_program(g, core, T, topo):
    route = T.tables["ROUTE"]
    n, off, pos = tables(route)
    r = topo.chip(core)
    k = core % 8
    base = core - k
    pl = plan(r, route)
    sem = T.sem
    sent = 0

    def dst_id(c):
        a = topo.addr(c)
        return DstId(rid=a[0], pnc=a[1])

    if k == RK:
        g.sync.dma_start(T.xs[:], T.x[:]).then_inc(sem.loaded, 16)
        ready, need = sem.loaded, 16
        g.wait_ge(ready, need)
        w = pl["width"]
        trs = []
        for i, h in enumerate([h for h in range(8) if h != RK]):
            s = pl["win"][h]
            trs.append(RemoteDMATransfer(dst_ids=[dst_id(base + h)], dma_engine_mask=3 << (2 * i),
                                         remote_sem=sem.chunk, src=T.xs[:, s:s + w], dst=T.xs[:, s:s + w]))
            sent += 2
        g.remote_dma_fused(trs, local_sem=sem.sent)
    else:
        ready, need = sem.chunk, 2
        g.wait_ge(ready, need)

    for w, trs in pl["calls"][k]:
        lst = []
        for t, mask, ne, dsts in trs:
            lst.append(RemoteDMATransfer(dst_ids=[dst_id(base + d[0]) for d in dsts], dma_engine_mask=mask,
                                         remote_sem=sem.packed, srcs=[T.xs[:, t:t + w]],
                                         dsts=[T[d[1]][:, d[2]:d[2] + w] for d in dsts]))
            sent += ne
        g.remote_dma_fused(lst, local_sem=sem.sent)
    queues = (g.sync, g.scalar)
    if pl["locs"][k]:
        for q in queues[:len(pl["locs"][k])]:
            q.wait_ge(ready, need)
    for i, (t, ln, buf, col) in enumerate(pl["locs"][k]):
        queues[i % 2].dma_start(T[buf][:, col:col + ln], T.xs[:, t:t + ln]).then_inc(sem.packed, 16)

    g.wait_ge(sem.packed, pl["packed"][k])
    for slot, e, cnt in pl["sends"][k]:
        dst = T.cores[e]
        a = topo.addr(dst)
        o = off[e][r]
        g.remote_dma(T.land[:, o:o + cnt], T["st%d" % slot][:, 0:cnt], sem.arrived, sem.sent, a[1], a[0], 0xFF)
        sent += 8

    if k == RK:
        g.sync.wait_ge(sem.packed, pl["packed"][k])
        g.sync.wait_ge(sem.arrived, 8 * (NR - 1))
        tot = off[r][NR]
        g.sync.dma_start(T.y[:, 0:tot], T.land[:, 0:tot]).then_inc(sem.stored, 16)
        g.sync.wait_ge(sem.stored, 16)
    g.wait_ge(sem.sent, sent)
